import numpy as np, ml_dtypes
CORES = [113,118,241,246]
N = 4
BF = ml_dtypes.bfloat16
V, M, W, TR, RO, CAP = 448, 224, 4096, 3, 3, 44
def spot(a, b, p, q):
    return ((a * (2 * b + 1) >> 4) + a + p * (2 * b + 613) + q * (2 * a + 37)) & (W - 1)
def look(X, a, b, p, q):
    return np.take_along_axis(X, spot(a, b, p, q).reshape(N, 8, 1, 16 * M), 3).reshape(N, 8, 16, 16, M)
def excess(R, z):
    return np.add.reduce(np.maximum(R - z[:, :, :, None, :], 0), axis=2)
def scan(X, G, B, d, z, t):
    ra = np.arange(N)[:, None, None, None]; ga = np.arange(8)[None, :, None, None]; z = z.astype(np.int32)
    n = np.add.reduce((G >= 0).astype(np.int64), axis=2)
    s = np.where((G >= 0) & ((G & 1) == (t & 1)), n[ra, ga, np.maximum(G, 0)], -1)
    e = np.take_along_axis(G, np.argmax(s, axis=2)[:, :, None, :], 2)[:, :, 0]
    e = np.where(np.max(s, axis=2) >= 0, e, -1)
    v = 2 * np.arange(M) + (t & 1); L = G[..., v]; on = L >= 0; a = np.maximum(L, 0)
    old = d[ra, ga, a]; mine = on & (e[ra, ga, a] == v); dv = d[:, :, v][:, :, None, :]
    new = old; pick = look(X, a, v, old, dv); low = excess(pick, z)
    for j in range(1, TR):
        p = (old + j) & 15; R = look(X, a, v, p, dv); x = excess(R, z); w = mine & (x < low)
        low = np.where(w, x, low); new = np.where(w, p, new); pick = np.where(w[:, :, None], R, pick)
    up = np.max(np.where(on[:, :, None], pick, 0), axis=3)
    o = np.take_along_axis(B, a, 3); both = np.concatenate([d, np.roll(d, -1, axis=0)], axis=2); do = both[ra, ga, o]
    dmg = np.where(on, excess(look(X, o, a, do, new), z) - excess(look(X, o, a, do, old), z), -99999)
    k = np.argmax(dmg, axis=2)[:, :, None, :]
    return n[:, :, v], v, L, a, mine, new, up, np.take_along_axis(dmg, k, 2)[:, :, 0], np.take_along_axis(o, k, 2)[:, :, 0]
def graph(rng, S, share):
    m = np.argsort(rng.random((S, V)), axis=1); i = np.arange(S)[:, None]; mate = np.zeros((S, V), np.int64)
    mate[i, m[:, :M]] = m[:, M:]; mate[i, m[:, M:]] = m[:, :M]
    act = 0.3 + 0.7 * rng.random(V); act[rng.random(V) < 0.04] = 0.0
    r = rng.random((S, V))[i, np.minimum(mate, np.arange(V))]
    return np.where(r < share * act * act[mate], mate, -1)
def tidy(tab):
    tab = np.array(tab, np.int64)
    for k in range(1, len(tab)): tab[k] = np.where(np.any(tab[:k] == tab[k], axis=0), -1, tab[k])
    tab = np.take_along_axis(tab, np.argsort(tab < 0, axis=0, kind="stable"), 0)[:16]
    return np.concatenate([tab, np.full((16 - len(tab), V), -1, np.int64)])
def plain(rng, share):
    return tidy(np.concatenate([np.where(rng.random((1, V)) < 0.15, np.arange(V), -1), graph(rng, 16, share)]))
def blocks(rng, own):
    p = rng.permutation(V).reshape(-1, 16); tab = np.zeros((16, V), np.int64)
    o = np.argsort(rng.random((len(p), 16, 16)), axis=2)
    tab[:, p.reshape(-1)] = p[np.arange(len(p))[:, None, None], o].reshape(-1, 16).T
    return tab if own else tidy(np.where(tab == np.arange(V), -1, tab))
def edges():
    return np.concatenate([np.arange(8), np.arange(V - 8, V)])
def corner(rng):
    c = edges(); tab = c[np.argsort(rng.random((16, V)), axis=0)]
    size = rng.choice(np.array([16, 16, 15, 14, 2, 0]), V); size[c] = rng.choice(np.array([16, 16, 15, 14]), 16)
    tab[:2, size == 2] = np.array([[0], [V - 1]])
    for u in (0, V - 1): tab[:, u] = np.concatenate([[V - 2], rng.permutation(c[c != V - 2])])
    tab[:, V - 2] = np.concatenate([[0], rng.permutation(c[1:15]), [V - 1]]); size[[0, V - 2, V - 1]] = 16
    return np.where(np.arange(16)[:, None] < size, tab, -1)
def lift(rng, rec, z, a, v, dv, o, do):
    def ex(x): return np.add.reduce(np.maximum(rec[:, x] - z.reshape((16,) + (1,) * (x.ndim - 1) + (-1,)), 0), axis=0)
    p = np.arange(16)[:, None]; E = ex(spot(a, v, p, dv))
    new = (p + np.argmin(np.stack([np.roll(E, -j, axis=0) for j in range(TR)]), axis=0)) & 15
    F = ex(spot(o[:, None], a, do[:, None], p))
    D = np.take_along_axis(F, np.broadcast_to(new, F.shape), 1) - F
    s = np.where(D > 0, 1 + rng.random(D.shape) + 2 * (np.arange(len(o))[:, None, None] == 0), 0)
    b = np.argmax(s.reshape(-1, s.shape[-1]), axis=0)
    return b & 15, b >> 4
def parts(rng):
    gl = np.stack([np.stack([plain(rng, float(rng.choice(np.array([0.7, 1.0, 1.5, 2.5])))) for g in range(8)]) for r in range(N)])
    rec = (256 * rng.random((N, 8, 16, W)) * (0.4 + 0.6 * rng.random((N, 8, 1, W)))).astype(np.int64)
    val = rng.integers(0, 16, (N, 8, V)); zl = (256 * rng.random((N, 8, 16, M)) ** 1.5).astype(np.int64)
    th = (rng.choice(np.array([4, 40, 200, 1000]), (N, 8, M)) * rng.random((N, 8, M))).astype(np.int64)
    gs = rng.choice(np.array([0.3, 0.5, 0.8]), (N, 8, 1, 1)); full = rng.integers(0, 8, N); gs[np.arange(N), full] = 1.0; th[np.arange(N), full] = rng.integers(0, 8, (N, M))
    nb = rng.integers(0, V, (N, 8, 16, V)) + V * (rng.random((N, 8, 16, V)) < gs)
    return rec, gl, nb, val, zl, th
def pack(rec, gl, nb, val, zl, th):
    return {"rec": rec.reshape(N, 128, W).astype(np.float32).astype(BF), "gl": np.ascontiguousarray(gl.reshape(N, 128, V)).astype(np.int32), "nb": np.ascontiguousarray(nb.reshape(N, 128, V)).astype(np.int32),
            "val": val.astype(np.int32), "zl": zl.reshape(N, 128, M).astype(np.float32).astype(BF), "th": th.astype(np.int32)}
def largest(rec, gl, nb, val, zl):
    return scan(rec.astype(np.int32), gl, nb, val, zl, 0)[7]
def tune(rng, top, want):
    pos = np.argsort(np.argsort(np.where(top > 0, rng.random(top.shape), 2.0), axis=2), axis=2); sel = (pos < want) & (top > 0); coin = rng.random(top.shape)
    low = np.where(coin < 0.5, top - 1, (rng.random(top.shape) * top).astype(np.int64))
    return np.where(sel, low, np.where(coin < 0.1, 4080, np.maximum(top, 0)))
def setup_inputs(rng):
    return pack(*parts(rng))
def setup_inputs_spread(rng):
    rec, gl, nb, val, zl, th = parts(rng)
    rec = (np.exp2(8 * rng.random((N, 8, 1, W))) * rng.random((N, 8, 16, W))).astype(np.int64)
    zl = (np.exp2(8 * rng.random((N, 8, 1, M))) * rng.random((N, 8, 16, M))).astype(np.int64)
    th = np.minimum((np.exp2(12 * rng.random((N, 8, M)) ** 1.5) - 1).astype(np.int64), 4080)
    nb = (2 * V * rng.random((N, 8, 16, V)) ** 1.5).astype(np.int64); val = (16 * rng.random((N, 8, V)) ** 2).astype(np.int64)
    return pack(rec, gl, nb, val, zl, th)
def setup_inputs_ends(rng):
    rec, gl, nb, val, zl, th = parts(rng)
    rec = 255 * np.where(rng.random((N, 8, 1, W)) < 0.8, rng.integers(0, 2, (N, 8, 1, W)), rng.integers(0, 2, (N, 8, 16, W)))
    val = 15 * rng.integers(0, 2, (N, 8, V)); th = 4080 * (rng.random((N, 8, M)) < 0.4).astype(np.int64)
    zl = 255 * np.where(rng.random((N, 8, 1, M)) < 0.6, rng.random((N, 8, 1, M)) < 0.35, rng.random((N, 8, 16, M)) < 0.35).astype(np.int64)
    e = rng.random((N, 8, 16, V)); nb = np.where(e < 0.4, 0, np.where(e < 0.85, 2 * V - 1, nb))
    for r in range(N):
        few = [6, 7] + [int(g) for g in rng.permutation(6)[:2]]
        for g in range(8):
            gl[r, g] = corner(rng) if g in few else tidy(np.concatenate([graph(rng, 14, 1.5), np.zeros((1, V), np.int64), np.full((1, V), V - 1, np.int64)]))
    for g in (6, 7):
        val[:, g, 0] = 15; val[:, g, V - 2] = 0; val[:, g, V - 1] = 0; zl[:, g, :, M - 1] = 0
        th[:, g, M - 1] = np.where(np.arange(N) % 2 == 1, 0, 4080)
        nb[:, g, 15, V - 1] = 2 * V - 1; nb[:, g, 0, 0] = 0 if g == 7 else 2 * V - 1
        hi = [spot(0, V - 2, 15, 0), spot(V - 1, V - 2, 0, 0), spot(2 * V - 1, V - 1, 0, 1), spot(0, 0, 15, 0) if g == 7 else spot(2 * V - 1, 0, 0, 15)]
        lo = [spot(0, V - 2, 0, 0), spot(V - 1, V - 2, 1, 0), spot(2 * V - 1, V - 1, 0, 0), spot(0, 0, 15, 15) if g == 7 else spot(2 * V - 1, 0, 0, 0)]
        for x in lo: rec[:, g, :, x] = 0
        for x in hi: rec[:, g, :, x] = 255
    return pack(rec, gl, nb, val, zl, th)
def setup_inputs_corners(rng):
    rec, gl, nb, val, zl, th = parts(rng); c = edges(); late = []
    for r in range(N):
        for g, k in enumerate(rng.permutation(8)):
            if k == 0:
                ev = np.concatenate([[V - 2], 2 * rng.permutation(M - 1)]); od = 2 * rng.permutation(M) + 1; h = M // 2
                tab = np.full((16, V), -1, np.int64)
                tab[0, ev[:h]] = od[:h]; tab[0, od[:h]] = ev[:h]; tab[0, od[h:]] = ev[:h]; tab[1, od[h:]] = ev[h:]; tab[0, ev[h:]] = od[h:]
                late.append((r, g, ev[:h], od[:h], od[h:]))
            elif k == 1: tab = blocks(rng, True)
            elif k == 2: tab = blocks(rng, False)
            elif k == 3:
                tab = graph(rng, 16, 2.0); tab = tidy(np.where((tab & 1 == 1) & (np.arange(V) & 1 == 1), tab, -1))
            elif k == 4:
                tab = graph(rng, 16, 2.0); off = rng.random(V) < 0.5; tab = tidy(np.where(off | off[tab], -1, tab))
            elif k == 5:
                tab = np.argsort(rng.random((V, V)), axis=1)[:, :16].T; tab = np.where(np.arange(16)[:, None] < rng.integers(0, 17, V), tab, -1)
            elif k == 6:
                tab = c[np.argsort(rng.random((16, V)), axis=0)]; tab[:, c] = np.argsort(rng.random((16, V)), axis=1)[:, :16].T
            else: tab = plain(rng, 1.5)
            gl[r, g] = tab
    m = np.arange(V); e = rng.integers(0, 10, (N, 8, 16, V))
    for k, x in enumerate((0, V - 1, V, 2 * V - 1, m, m + V)): nb = np.where(e == k, x, nb)
    e = rng.integers(0, 4, (N, 8, V)); val = np.where(e == 0, 0, np.where(e == 1, 15, val))
    e = rng.integers(0, 6, (N, 8, 1, M)); zl = np.where(e == 0, 0, np.where(e == 1, 255, zl >> 1))
    want = rng.choice(np.array([0, 1, CAP - 1, CAP, CAP + 1, M]), (N, 8, 1))
    for r, g, v, a, o in late:
        zl[r, g, :, M - 1] = 0; dv = val[r, g, v]; do = val[r, g, o]; q = (np.arange(16) + 1) & 15
        x = spot(a[0], v[0], np.arange(16), dv[0]); y = spot(o[0], a[0], do[0], np.arange(16))
        s = int(np.argmax((x != y) & (x[q] != y[q]))); u = int(q[s])
        rec[r, g, :, int(x[s])] = 255; rec[r, g, :, int(y[u])] = 255; rec[r, g, :, int(x[u])] = 0; rec[r, g, :, int(y[s])] = 0
        p = lift(rng, rec[r, g], zl[r, g][:, v >> 1], a, v, dv, o[None], do[None])[0]
        val[r, g, a] = p; val[r, g, a[0]] = s; nb[r, g][:, a] = o; want[r, g, 0] = M
    th = tune(rng, largest(rec, gl, nb, val, zl), want)
    for r, g, v, a, o in late: th[r, g, M - 1] = 4079
    return pack(rec, gl, nb, val, zl, th)
def setup_inputs_crowd(rng):
    rec, gl, nb, val, zl, th = parts(rng); zl = zl >> 1; ev = 2 * np.arange(M)
    spots = np.array([V, 2 * V - 1, V + M]); cnt = np.array([CAP, CAP + 1, CAP - 1, M, CAP + 1]); want = np.zeros((N, 8, 1), np.int64)
    for r in range(N):
        most = ((2, 3), (4, 5), (3, 2), (5, 4))[r % 4]
        left = [g for g in range(1, 8) if g not in most]
        want[r, left, 0] = cnt if r == 0 else rng.permutation(cnt)
        want[r, most[0], 0] = M; want[r, most[1], 0] = M - 1
        for g in range(8):
            gl[r, g] = plain(rng, 1.5); s = int(rng.choice(spots))
            if g in most:
                od = 2 * rng.permutation(M) + 1; tab = np.full((16, V), -1, np.int64); tab[0, ev] = od; tab[0, od] = ev; gl[r, g] = tab
                o = np.tile(rng.permutation(spots)[:, None], (1, M))
                p, k = lift(rng, rec[r, g], zl[r, g], od, ev, val[r, g, ev], o, val[(r + 1) % N, g][o - V])
                val[r, g, od] = p; nb[r, g] = o[0, 0]; nb[r, g][:, od] = o[k, np.arange(M)]
            elif g == 0: nb[r, g] = (0, V - 1)[r % 2]
            elif g < 5: nb[r, g] = s
            elif g == 5: nb[r, g] = rng.choice(spots, (16, V))
            else: nb[r, g] = np.where(rng.random((16, V)) * CAP < 1, 2 * V - 1 if s == V else V, s)
    top = largest(rec, gl, nb, val, zl); got = np.minimum(np.add.reduce((top > 0).astype(np.int64), axis=2), want[:, :, 0])
    for r in range(N): want[r, 0, 0] = ((31, 0)[r % 2] - int(np.add.reduce(got[r, 1:]))) & 31
    return pack(rec, gl, nb, val, zl, tune(rng, top, want))
def check_inputs(d):
    bad = []
    for k, lo, hi in (("rec", 0, 255), ("gl", -1, V - 1), ("nb", 0, 2 * V - 1), ("val", 0, 15), ("zl", 0, 255), ("th", 0, 4080)):
        x = np.asarray(d[k]).astype(np.float64)
        if not (np.min(x) >= lo and np.max(x) <= hi): bad.append("range of " + k)
        if np.any(x != np.floor(x)): bad.append("whole numbers in " + k)
    g = np.asarray(d["gl"]).reshape(N, 8, 16, V); on = g >= 0; s = np.sort(g, axis=2)
    if np.any(on[:, :, 1:] & ~on[:, :, :-1]): bad.append("gl: a name after an empty slot")
    if np.any((s[:, :, 1:] == s[:, :, :-1]) & (s[:, :, 1:] >= 0)): bad.append("gl: a name twice in one list")
    return bad
def reference(rec, gl, nb, val, zl, th):
    X = rec.astype(np.float32).astype(np.int32).reshape(N, 8, 16, W); G = gl.astype(np.int64).reshape(N, 8, 16, V); B = nb.astype(np.int64).reshape(N, 8, 16, V)
    d = val.astype(np.int64); z = zl.astype(np.float32).astype(np.int32).reshape(N, 8, 16, M); h = th.astype(np.int64); c = np.zeros((N, 1, 1), np.int64)
    for t in range(RO):
        n, v, L, a, mine, new, up, top, who = scan(X, G, B, d, z, t)
        hurt = top > h + (c & 31)
        c = np.add.reduce(hurt.astype(np.int64).reshape(N, 8 * M), axis=1).reshape(N, 1, 1)
        z = np.roll((z + up) >> 1, 1 + t, axis=0)
        w = np.nonzero(mine); d = d + 0; d[w[0], w[1], a[w]] = new[w]
        gh = (hurt & (who >= V)).astype(np.int64); told = (gh == 1) & (np.add.accumulate(gh, axis=2) - gh < CAP)
        w = np.nonzero(told); np.add.at(d, ((w[0] + 1) % N, w[1], who[w] - V), 1); d = d & 15
        w = np.nonzero(hurt & (who < V) & (n < 16) & ~np.any(L == who[:, :, None, :], axis=2))
        G[w[0], w[1], n[w], v[w[2]]] = who[w]
    return {"yl": G.reshape(N, 128, V).astype(np.float32), "yd": d.astype(np.float32), "yz": z.reshape(N, 128, M).astype(np.float32).astype(BF)}

from concourse.mybir import AluOpType, AxisListType, ActivationFunctionType

V, M, W, RO, CAP = 448, 224, 4096, 3, 44
CELLS = 16 * M
WIN = CELLS + V
CH = 1792


def bf(n): return ("sbuf", [128, n], "bfloat16")
def f4(n): return ("sbuf", [128, n], "float32")
def i4(n): return ("sbuf", [128, n], "int32")
def u2(n): return ("sbuf", [128, n], "uint16")


SCRATCH = {
    "GI": i4(V), "NBI": i4(V), "VI": ("sbuf", [8, V], "int32"), "THI": ("sbuf", [8, M], "int32"), "Z0": bf(M),
    "REC": bf(W + 16), "NW": bf(2 * CELLS), "KW": bf(2 * CELLS), "KC": bf(464), "KT": bf(2 * CH), "WR": bf(WIN), "WP": bf(WIN),
    "GF": f4(464), "GU": u2(V), "G0": bf(V), "NBD": bf(2 * V), "NBT": i4(2 * V),
    "VB": ("sbuf", [8, V], "bfloat16"), "THT": ("sbuf", [8, 2 * M], "int32"), "THB": ("sbuf", [8, 2 * M], "bfloat16"),
    "TN": bf(464), "X34": bf(1024), "TE": bf(912), "ID": bf(912),
    "IOQ": i4(8), "COL": f4(32), "IOM": f4(128), "IOX": f4(464), "IOC": f4(28), "S1": f4(4 * M), "IO8": f4(16),
    "RA": bf(CH), "RM": bf(CH), "CK": bf(512), "J84": bf(84), "PATP": f4(256), "PATC": f4(V), "LPI": i4(16),
    "LPC": u2(44), "SELS": bf(64), "ONE": bf(128), "UPR": bf(128), "IDN": bf(128), "E8": ("sbuf", [8, 128], "bfloat16"),
    "EJ": ("sbuf", [32, 128], "bfloat16"), "EE0": ("sbuf", [32, 128], "bfloat16"), "EE": ("sbuf", [32, 2048], "bfloat16"),
    "BD": bf(128), "MM": bf(1024),
    "LW": bf(2048), "LW4": bf(2048), "LWE0": bf(2048), "LWE1": bf(2048), "LWD": bf(2048), "LWN": bf(2048),
    "LWK": bf(2048), "LWO": bf(2048), "DA2": bf(2048), "W32": f4(32), "B32": f4(32), "TH0": f4(32), "THC": f4(32),
    "MAT": bf(V), "NG": bf(V), "INL": bf(V), "MSK": bf(2 * V), "OG": bf(V), "OA": f4(V), "NVO": bf(2 * V), "KV": bf(V),
    "PAY": bf(V), "GD": bf(2 * V), "ZE": bf(V), "MT": bf(3 * V), "RP": bf(V), "MN": bf(V), "MO": bf(V), "NMO": bf(V),
    "SI": i4(M), "SF": f4(6 * M), "ISL": u2(M), "OHN": f4(M), "UPD": f4(M), "ZH": f4(M), "ZI": i4(M),
    "SC": f4(512), "IT": f4(14 * 32), "II": i4(4 * 32), "IBC": bf(64), "XX": bf(64), "XT": ("sbuf", [32, M], "bfloat16"),
    "OHP": bf(256), "OHC": bf(V), "DT": bf(64), "CF": f4(4), "CI": i4(4),
    "DF": f4(28 * 104), "DN": i4(28 * 72), "DU": u2(28 * 64), "DB": bf(32 * 12),
    "PA": ("psum", [128, 512], "float32"), "PB": ("psum", [128, 512], "float32"), "PC": ("psum", [128, 512], "float32"),
    "PD": ("psum", [128, 512], "float32"), "PK": ("psum", [128, 512], "float32"), "PN": ("psum", [128, 512], "float32"),
    "PS": ("psum", [128, 512], "float32"), "PJ": ("psum", [128, 512], "float32"),
}
for _t in range(3):
    SCRATCH["WD%d" % _t] = bf(WIN)
    SCRATCH["LG%d" % _t] = bf(32)
    SCRATCH["LN%d" % _t] = bf(32)
    SCRATCH["LZ%d" % _t] = bf(M)
    SCRATCH["ZB%d" % _t] = bf(M)
SEMAPHORES = ["cv", "cs", "ct", "cg"] + ["dma%d" % k for k in range(40)] + ["rg%d" % k for k in range(3)] + \
    ["rn%d" % k for k in range(3)] + ["rz%d" % k for k in range(3)] + ["ls%d" % k for k in range(9)]
ALIAS = {"SELD": ("SELS", 0), "SELP": ("SELS", 16), "SELT": ("SELS", 32), "SELU": ("SELS", 48), "IB": ("IBC", 0), "CB": ("IBC", 32),
         "LP": ("LPC", 0), "LC": ("LPC", 16), "R2B": ("MM", 0), "LOA": ("MM", 128), "IP": ("MM", 256), "N0W": ("MM", 384),
         "N1W": ("MM", 512), "I3": ("MM", 640), "I4": ("MM", 768), "YD": ("SF", 0), "YL": ("SF", 448)}
PSUM = {"PA", "PB", "PC", "PD", "PK", "PN", "PS", "PJ"}


def builder(g, T):
    eng = {"v": g.vector, "s": g.scalar, "t": g.tensor, "g": g, "y": g.sync}
    cnt = {"v": 0, "s": 0, "t": 0, "g": 0, "dma": 0, "ls": 0}
    known = {q: {} for q in eng}
    log = {}
    total = {}

    def wait(q, evs):
        k = known[q]
        top = {}
        for e in evs:
            if k.get(e[0], 0) < e[1] and (e[0] not in top or top[e[0]][1] < e[1]): top[e[0]] = e
        for e in sorted(top.values(), key=lambda e: -sum(e[2].values())):
            if k.get(e[0], 0) >= e[1]: continue
            eng[q].wait_ge(T.sem[e[0]], e[1])
            k[e[0]] = e[1]
            for s, n in e[2].items():
                if k.get(s, 0) < n: k[s] = n

    def deps(q, outs, ins, comp):
        evs = []
        for regs, w in ((ins, False), (outs, True)):
            for b, lo, hi in regs:
                for r in log.get(b, []):
                    same = comp and r[3] == q
                    if b in PSUM:
                        if not same or (q != "t" and (w or r[2])): evs.append(r[4])
                    elif r[0] < hi and lo < r[1] and (w or r[2]):
                        if same and (q == "t" or not r[2]): continue
                        evs.append(r[4])
        return evs

    def note(q, outs, ins, ev):
        for regs, w in ((ins, False), (outs, True)):
            for b, lo, hi in regs:
                L = log.setdefault(b, [])
                if b in PSUM: L[:] = [r for r in L if r[3] != q or r[2] != w]
                else: L[:] = [r for r in L if not (lo <= r[0] and r[1] <= hi and (w or (not r[2] and r[3] == q and q in "vstg")))]
                L.append((lo, hi, w, q, ev))

    def emit(q, outs, ins, call):
        wait(q, deps(q, outs, ins, True))
        cnt[q] += 1
        s = "c" + q
        call().then_inc(T.sem[s], 1)
        total[s] = cnt[q]
        note(q, outs, ins, (s, cnt[q], dict(known[q])))

    def dma(q, out, in_):
        wait(q, deps("d" + q, out[1], in_[1], False))
        s = "dma%d" % cnt["dma"]
        cnt["dma"] += 1
        eng[q].dma_start(out[0], in_[0]).then_inc(T.sem[s], 16)
        total[s] = 16
        note("d" + s, out[1], in_[1], (s, 16, dict(known[q])))

    def send(out, in_, sem, to):
        wait("g", deps("r", [], in_[1], False))
        s = "ls%d" % cnt["ls"]
        cnt["ls"] += 1
        g.remote_dma(out[0], in_[0], T.sem[sem], T.sem[s], to[1], to[0], to[2])
        total[s] = to[3]
        note("r" + s, [], in_[1], (s, to[3], dict(known["g"])))

    def arrive(view, sem, n):
        total[sem] = n
        for b, lo, hi in view[1]: log.setdefault(b, []).append((lo, hi, True, "x" + sem, (sem, n, {})))

    def finish():
        wait("y", [(s, n, {}) for s, n in sorted(total.items())])

    return emit, dma, send, arrive, finish


def rank_program(g, core, T, topo):
    rank = T.rank_of(core)
    if rank is None: return
    N = len(T.cores)
    A, F = AluOpType, ActivationFunctionType
    emit, dma, send, arrive, finish = builder(g, T)

    def B(n, lo, hi, st=1, p=128):
        if n in ALIAS: n, lo, hi = ALIAS[n][0], lo + ALIAS[n][1], hi + ALIAS[n][1]
        ap = T[n][0:p, lo:hi] if st == 1 else T[n][0:p, lo:hi:st]
        return (ap, [(n, lo, hi)])

    def P4(n, p0, p1, lo, hi): return (T[n][p0:p1, lo:hi], [(n, lo, hi)])
    def ind(win, off): return (win[0].indirect(off[0]), win[1] + off[1])
    def num(s): return (s, []) if s is None or isinstance(s, (int, float)) else s
    def tt(o, a, b, op): emit("v", o[1], a[1] + b[1], lambda: g.vector.tensor_tensor(o[0], a[0], b[0], op))
    def cp(o, a): emit("v", o[1], a[1], lambda: g.vector.tensor_copy(o[0], a[0]))

    def ts(o, a, s1, op0, s2=None, op1=None):
        x, y = num(s1), num(s2)
        if op1 is None: emit("v", o[1], a[1] + x[1], lambda: g.vector.tensor_scalar(o[0], a[0], x[0], None, op0))
        else: emit("v", o[1], a[1] + x[1] + y[1], lambda: g.vector.tensor_scalar(o[0], a[0], x[0], y[0], op0, op1))

    def scan(o, a, b, op0, op1): emit("v", o[1], a[1] + b[1], lambda: g.vector.tensor_tensor_scan(o[0], a[0], b[0], 0.0, op0, op1))
    def fill(o, c): emit("v", o[1], [], lambda: g.vector.memset(o[0], c))

    def act(o, a, scale=1.0, bias=0.0, relu=False):
        x, y = num(scale), num(bias)
        fn = F.Relu if relu else F.Copy if y[0] == 0.0 and not y[1] else F.Identity
        emit("s", o[1], a[1] + x[1] + y[1], lambda: g.scalar.activation(o[0], a[0], fn, bias=y[0], scale=x[0]))

    def mm(o, l, r, start, stop): emit("t", o[1], l[1] + r[1], lambda: g.tensor.matmul(o[0], l[0], r[0], start, stop))
    def iota(o, pat, base, cm): emit("g", o[1], [], lambda: g.iota(o[0], pat, base, cm, allow_small_or_imprecise_dtypes=True))
    def asel(o, a, pat, op, base, cm): emit("g", o[1], a[1], lambda: g.affine_select(o[0], a[0], pat, op, 0.0, base, cm))
    def mat(n, p, k=128): return (T[n][0:k, p * 128:p * 128 + 128], [(n, p * 128, p * 128 + 128)])

    def dist(o, n, src, base, st, cols, first=True):
        for p in range(16):
            lo = base + p
            mm(o, mat(n, p), B(src, lo, lo + (cols - 1) * st + 1, st), first and p == 0, p == 15)

    def spread(src, first):
        for p in range(16): mm(B("PA", p, p + 433, 16), mat("DA2", p), src, first, first or p == 15)

    slots = {}

    def slot(buf, width):
        def f(name):
            k = (buf, name[:-1] + "0" if name[-1] == "2" and buf != "DB" else name)
            if k not in slots: slots[k] = sum(1 for x in slots if x[0] == buf)
            return B(buf, slots[k] * width, slots[k] * width + 28)
        return f

    DF, DN, DU, DB = slot("DF", 28), slot("DN", 28), slot("DU", 28), slot("DB", 32)

    def wide(f, n, s):
        vs = [f("%s%d%s" % (n, j, s)) for j in range(3)]
        return B(vs[0][1][0][0], vs[0][1][0][1], vs[2][1][0][2])

    def out32(name):
        b, lo, hi = DB(name)[1][0]
        return B(b, lo, lo + 32)

    def lanes(src, dst): return topo.engines(src, dst)[:8]

    def route(dst):
        c = T.cores[dst % N]
        rid, pid = topo.addr(c, core)
        return (rid, pid, sum(1 << e for e in lanes(core, c)), len(lanes(core, c)))

    def came(src, view, sem): arrive(view, sem, len(lanes(T.cores[src % N], core)))

    col = lambda j, p=128: B("COL", j, j + 1, 1, p)
    dma("y", B("GI", 0, V), (T.gl[:, :], []))
    dma("y", B("VI", 0, V, 1, 8), (T.val[:, :], []))
    dma("y", B("NBI", 0, V), (T.nb[:, :], []))
    dma("y", B("Z0", 0, M), (T.zl[:, :], []))
    dma("y", B("REC", 0, W), (T.rec[:, :], []))
    dma("y", B("THI", 0, M, 1, 8), (T.th[:, :], []))
    for t in range(3):
        came(rank + 1, B("LG%d" % t, 0, 32), "rg%d" % t)
        came(rank - 1, B("LN%d" % t, 0, 32), "rn%d" % t)
        came(rank - 1 - t, B("LZ%d" % t, 0, M), "rz%d" % t)
    iota(B("IOQ", 0, 1), [[0, 1]], 0, 1)
    iota(B("IOM", 0, 128), [[1, 8], [0, 16]], 0, 0)
    fill(B("ONE", 0, 128), 1.0)
    fill(B("WD0", 0, CH), 0.0)
    asel(B("IDN", 0, 128), B("ONE", 0, 128), [[1, 128]], A.is_equal, 0, -1)
    iota(B("X34", 0, 512), [[256, 2], [0, 256]], 0, 0)
    iota(B("X34", 512, 1024), [[0, 2], [1, 256]], 0, 0)
    iota(B("IOX", 0, 464), [[1, 464]], 0, 0)
    asel(B("E8", 0, 128, 1, 8), B("ONE", 0, 128, 1, 8), [[1, 128]], A.is_equal, -2, -16)
    iota(B("IOC", 0, 28), [[16, 28]], 0, 0)
    ts(B("IOQ", 1, 2), B("IOQ", 0, 1), 15, A.bitwise_and)
    ts(B("IOQ", 2, 3), B("IOQ", 0, 1), 4, A.arith_shift_right)
    cp(col(0), B("IOQ", 1, 2))
    cp(col(1), B("IOQ", 2, 3))
    ts(B("BD", 0, 128), B("IOM", 0, 128), col(1), A.is_equal)
    for j in range(5): ts(col(4 + j), col(0), float(j), A.is_equal)
    ts(col(9), col(4), -128.0, A.mult)
    ts(col(11), col(5), -256.0, A.mult, col(9), A.add)
    ts(col(10), col(4), -256.0, A.mult)
    ts(col(14), col(5), -128.0, A.mult, col(10), A.add)
    ts(col(17), col(4), col(5), A.add)
    ts(B("TN", 0, 1), col(17), -256.0, A.mult)
    fill(B("TN", V + 1, 464), 0.0)
    fill(B("N0W", 0, 256), 0.0)
    ts(B("N0W", 0, 113, 16), B("BD", 0, 113, 16), 16.0, A.mult)
    ts(B("N1W", 1, 114, 16), B("BD", 0, 113, 16), 16.0, A.mult)
    ts(B("R2B", 0, 128), B("BD", 0, 128), col(6), A.mult)
    ts(B("I3", 0, 128), B("IDN", 0, 128), col(7), A.mult)
    ts(B("I4", 0, 128), B("IDN", 0, 128), col(8), A.mult)
    ts(B("G0", 0, V), B("GI", 0, V), 0.0, A.is_ge)
    ts(B("GU", 0, M), B("GI", 0, V - 1, 2), 1.0, A.add)
    ts(B("GU", M, V), B("GI", 1, V, 2), 1.0, A.add)
    cp(B("VB", 0, V, 1, 8), B("VI", 0, V, 1, 8))

    def sizes(last):
        mm(B("PA", 0, V), B("I3", 0, 128), B("X34", 1, V + 1), True, False)
        mm(B("PA", 0, V), B("I4", 0, 128), B("X34", 513, 513 + V), False, False)
        mm(B("PA", 0, V - 1, 2), B("N0W", 0, 128), B("G0", 0, V - 1, 2), False, False)
        mm(B("PA", 1, V, 2), B("N1W", 0, 128), B("G0", 1, V, 2), False, last)

    sizes(False)
    mm(B("PA", 0, V), B("E8", 0, 128, 1, 8), B("VB", 0, V, 1, 8), False, True)
    ts(B("TN", 1, V, 2), B("PA", 0, V - 1, 2), col(11), A.add)
    ts(B("TN", 2, V + 1, 2), B("PA", 1, V, 2), col(14), A.add)
    TNW = B("TN", 0, 464)

    def table(values, alone=False):
        if alone:
            spread(B("DT", 0, 28), True)
            act(B("TN", 1, V + 1), B("PA", 0, V))
            return
        sizes(not values)
        if values: spread(B("DT", 0, 28), False)
        act(B("TN", 1, V, 2), B("PA", 0, V - 1, 2), bias=col(11))
        act(B("TN", 2, V + 1, 2), B("PA", 1, V, 2), bias=col(14))

    def sgather(c0, c1): act(B("KW", 16 * c0, 16 * c1), ind(TNW, B("GU", c0, c1)))
    def vgather(c0, c1): cp(B("KW", 16 * c0, 16 * c1), ind(TNW, B("GU", c0, c1)))
    turn = [0]

    def half():
        turn[0] ^= 1
        return turn[0] * CH

    def scans(lo, hi):
        while lo < hi:
            n, b = min(CH, hi - lo), half()
            scan(B("KT", b, b + n), B("RA", 0, n), B("KW", lo, lo + n), A.add, A.max)
            cp(B("KC", lo // 16, (lo + n) // 16), B("KT", b + 15, b + n, 16))
            lo += n

    CUT = 320
    for c in range(0, CUT, 80): sgather(c, c + 80)
    fill(B("LW", 0, 2048), 0.0)
    for a in range(8): cp(B("LW", 16 * a, 16 * a + 129 * 15 + 1, 129), B("BD", 16 * a, 16 * a + 16))
    for n, op, b in (("LWD", A.is_equal, -2), ("LWN", A.is_ge, -3)):
        asel(B(n, 0, 2048), B("LW", 0, 2048), [[0, 16], [-16, 8], [0, 16]], op, b, 1)
    iota(B("SF", 0, 912), [[0, 57], [1, 16]], 0, 0)
    asel(B("LWE1", 0, 2048), B("LW", 0, 2048), [[0, 16], [-16, 8], [0, 16]], A.is_equal, -1, 1)
    for j, b in enumerate((1, 3, 613, 615)): iota(B("S1", j * M, j * M + M), [[4, M]], b, 0)
    fill(B("RA", 0, CH), 1.0)
    fill(B("RA", 0, CH - 15, 16), -512.0)
    fill(B("KC", V, 464), 0.0)
    vgather(CUT, 448)
    for n, m in (("NW", 4), ("WP", 2), ("WD1", 2), ("WD2", 2)):
        for j in range(m): dma("y", B(n, j * CH, j * CH + CH), B("WD0", 0, CH))
    dma("y", B("WD0", CH, 2 * CH), B("WP", CH, 2 * CH))
    scans(16 * CUT, 7168)
    aD = DF("aD")
    ts(aD, B("IOC", 0, 28), col(0), A.add)
    ts(DF("A37"), aD, 2.0, A.mult, 37.0, A.add)
    ts(DF("A1"), aD, 2.0, A.mult, 1.0, A.add)
    ts(DF("A613"), aD, 2.0, A.mult, 613.0, A.add)
    ts(DF("CNB"), aD, -448.0, A.add)
    ts(DF("CPOS"), aD, float(CELLS), A.add)
    ts(B("IOQ", 5, 6), B("IOQ", 0, 1), 1, A.bitwise_and)
    ts(col(3), B("IOQ", 5, 6), 3576.0, A.mult, 15.0, A.add)
    ts(DF("CM"), aD, 8.0, A.mult, col(3), A.add)
    ts(col(2), col(0), 1.0, A.add)
    for j, x in ((28, -1.0), (29, 35.0), (30, 8192.0)): fill(col(j), x)
    ts(col(9), col(4), 16.0, A.mult, col(5), A.add)
    act(B("LWE0", 0, 2048), B("LW", 0, 2048), scale=col(4))
    act(B("LWK", 0, 2048), B("LW", 0, 2048), scale=col(2))
    scans(0, 16 * CUT)

    def base1(rows):
        for p in range(16):
            lo = (p & 1) * M + (p >> 1)
            mm(B("PB", 0, 28), mat(rows, p), B("KC", lo, lo + 27 * 8 + 1, 8), p == 0, p == 15)

    def base2(nm):
        ts(DN("kI" + nm), B("PB", 0, 28), 128.0, A.add)
        ts(DF("val" + nm), B("PB", 0, 28), -200.0, A.is_gt)
        ts(DN("r" + nm), DN("kI" + nm), 15, A.bitwise_and)
        tt(DN("ce" + nm), DF("CM"), DN("r" + nm), A.subtract)
        cp(DU("ce" + nm), DN("ce" + nm))
        act(B("NG", 0, V), ind(B("KW", 0, 7168), DU("ce" + nm)))
        dist(B("PB", 32, 60), "LWN", "NG", 0, 16, 28)

    def base3(nm, e): tt(e, B("PB", 32, 60), DF("val" + nm), A.mult)

    def send_moved(t): send(B("LG%d" % t, 0, 32), out32("mv%d" % t), "rg%d" % t, route(rank + N - 1))
    def zin(t): return B("Z0", 0, M) if t == 0 else B("LZ%d" % (t - 1), 0, M)
    def rec(u): return ind(B("REC", 0, W + 16), DU(u))

    def E1(t):
        s = str(t)
        e1, em, ei = DF("e" + s), DN("em" + s), DN("ei" + s)
        cp(DU("e" + s), e1)
        act(B("MSK", 0, V), ind(B("ID", 0, 912), DU("e" + s)))
        ts(em, e1, -1.0, A.add)
        ts(DN("ec" + s), em, 4, A.arith_shift_right)
        cp(DU("ec" + s), DN("ec" + s))
        ts(ei, em, 1, A.arith_shift_right)
        cp(DU("ei" + s), ei)

    def E2(t):
        s = str(t)
        tt(B("MAT", 0, V), ind(B("GF", 0, 464), DU("e" + s)), B("IOX", 1, V + 1), A.is_equal)
        dist(B("PB", 64, 92), "LWK", "MAT", 0, 16, 28)
        ts(DF("s1" + s), DF("e" + s), 2.0, A.mult, -1.0, A.add)
        tt(DN("m1" + s), DF("s1" + s), aD, A.mult)
        ts(DN("m2" + s), DN("m1" + s), 4, A.arith_shift_right)
        tt(DF("c1" + s), DN("m2" + s), aD, A.add)
        ts(DF("sl0" + s), DF("s1" + s), 612.0, A.add)

    def E3(t):
        s = str(t)
        ts(DF("nk" + s), B("PB", 64, 92), 448.0, A.mult)
        cp(DF("kk" + s), B("PB", 64, 92))
        tt(DF("nk" + s), DF("nk" + s), DF("CNB"), A.add)
        cp(DU("nk" + s), DF("nk" + s))
        act(B("OG", 0, V), ind(B("NW", 0, 7168), DU("nk" + s)))
        dist(B("PB", 96, 124), "LWO", "OG", 0, 16, 28)

    def E4(t):
        s = str(t)
        ts(DF("mi" + s), DF("kk" + s), 0.5, A.is_gt)
        t1 = DF("ps" + s)
        ts(t1, DN("ei" + s), 16.0, A.mult, -1.0 - CELLS, A.add)
        tt(t1, t1, DF("kk" + s), A.add)
        tt(t1, t1, aD, A.subtract)
        tt(t1, t1, DF("mi" + s), A.mult)
        tt(t1, t1, DF("CPOS"), A.add)
        cp(DU("ps" + s), t1)

    def E5a(t):
        s = str(t)
        ts(DU("o" + s), B("PB", 96, 124), 1.0, A.add)
        act(B("MSK", V, 2 * V), ind(B("ID", 0, 912), DU("o" + s)))

    def E5b(t):
        s = str(t)
        cp(DN("o" + s), B("PB", 96, 124))
        ts(DN("oc" + s), DN("o" + s), 4, A.arith_shift_right)
        cp(DU("oc" + s), DN("oc" + s))
        tt(DN("om" + s), DN("o" + s), DF("A1"), A.mult)
        ts(DN("om" + s), DN("om" + s), 4, A.arith_shift_right)
        tt(DF("ob" + s), DN("om" + s), DN("o" + s), A.add)
        ts(DF("s37" + s), DN("o" + s), 2.0, A.mult, 37.0, A.add)

    def D1(t):
        s = str(t)
        tt(B("GD", 0, V), ind(B("DT", 0, 64), DU("ec" + s)), B("MSK", 0, V), A.mult)
        dist(B("PD", 0, 28), "LW", "GD", 0, 16, 28)
        for j in range(3): ts(DN("pj%d%s" % (j, s)), DN("d" + s), float(j), A.add)
        pj = wide(DN, "pj", s)
        ts(pj, pj, 15, A.bitwise_and)

    def D2(t):
        s = str(t)
        for j in range(3): tt(DF("bs%d%s" % (j, s)), DN("pj%d%s" % (j, s)), DF("sl0" + s), A.mult)
        tt(DF("qt" + s), B("PD", 0, 28), DF("A37"), A.mult)
        tt(DF("c0" + s), DF("c1" + s), DF("qt" + s), A.add)
        for j in range(3): tt(DN("ix%d%s" % (j, s)), DF("bs%d%s" % (j, s)), DF("c0" + s), A.add)
        ix = wide(DN, "ix", s)
        ts(ix, ix, 4095, A.bitwise_and)
        cp(wide(DU, "ix", s), ix)

    def D3(t):
        tt(B("GD", V, 2 * V), ind(B("DT", 0, 64), DU("oc%d" % t)), B("MSK", V, 2 * V), A.mult)
        dist(B("PC", 128, 156), "LW", "GD", V, 16, 28)

    def ze(t): act(B("ZE", 0, V), ind(zin(t), DU("ei" + str(t))))
    def R1(t, j): tt(B("MT", j * V, j * V + V), rec("ix%d%d" % (j, t)), B("ZE", 0, V), A.max)

    def R1x(t):
        mm(B("PC", 0, 84), B("IDN", 0, 128), B("J84", 0, 84), True, False)
        dist(B("PC", 0, 84), "LW4", "MT", 0, 16, 84, first=False)

    def D4(t):
        s = str(t)
        tt(DF("od" + s), B("PC", 128, 156), DF("A613"), A.mult)
        tt(DF("co" + s), DF("ob" + s), DF("od" + s), A.add)
        tt(DF("ot" + s), DN("d" + s), DF("s37" + s), A.mult)
        tt(DN("io" + s), DF("ot" + s), DF("co" + s), A.add)
        ts(DN("io" + s), DN("io" + s), 4095, A.bitwise_and)
        cp(DU("io" + s), DN("io" + s))

    def R2(t):
        tt(B("MO", 0, V), rec("io%d" % t), B("ZE", 0, V), A.max)
        act(B("NMO", 0, V), B("MO", 0, V), scale=-1.0)

    def R3(t):
        s = str(t)
        cp(DF("x" + s), B("PC", 0, 28))
        tt(DF("x" + s), B("PC", 28, 56), DF("x" + s), A.min)
        tt(DN("x" + s), B("PC", 56, 84), DF("x" + s), A.min)
        ts(DN("x" + s), DN("x" + s), 3, A.bitwise_and)
        tt(DF("jm" + s), DN("x" + s), DF("mi" + s), A.mult)
        tt(DN("np" + s), DF("jm" + s), DN("d" + s), A.add)
        nd = DN("nd" + s)
        ts(nd, DN("np" + s), 15, A.bitwise_and)
        for a, b, c, d in (("nt", "s37", "co", "in"), ("pt", "sl0", "c0", "ip")):
            tt(DF(a + s), nd, DF(b + s), A.mult)
            tt(DN(d + s), DF(a + s), DF(c + s), A.add)
            ts(DN(d + s), DN(d + s), 4095, A.bitwise_and)
            cp(DU(d + s), DN(d + s))
            if d == "in": tt(B("MN", 0, V), rec("in" + s), B("ZE", 0, V), A.max)
        act(B("RP", 0, V), rec("ip" + s), scale=0.5)
        wd = "WD" + s
        emit("v", [(wd, 0, WIN)], [("MN", 0, V), ("NMO", 0, V)] + DU("ps" + s)[1],
             lambda: g.vector.tensor_tensor(T[wd][:, 0:WIN].indirect(DU("ps" + s)[0]), T["MN"][:, 0:V], T["NMO"][:, 0:V], A.add))
        if t < 2:
            cp(DB("mv%d" % (t + 1)), nd)
            send_moved(t + 1)

    def open_keys(): mm(B("PK", 0, 512), B("IDN", 0, 128), B("CK", 0, 512), True, False)

    def keys(w, sel, stop):
        for h in range(2):
            for k in range(16):
                lo = h * 112 * 16 + k
                o = (T["PK"][0:112, h * 256 + k:h * 256 + 241 + k:16], [("PK", 0, 512)])
                mm(o, B(w, lo, lo + 111 * 16 + 1, 16), B(sel, 0, 16), False, stop and h == 1 and k == 15)

    def F1(t):
        s, par = str(t), t & 1
        if t == 2: return
        mm(B("PA", 0, V), B("N0W", 0, 128), B("G0", 0, V), True, True)
        act(B("TE", 1, V + 1), B("PA", 0, V))
        act(B("NVO", 0, V), ind(B("TE", 0, 912), DU("e" + s)))
        ts(DU("kc" + s), DN("ei" + s), float(par * M), A.add)

    def F1b(t):
        if t < 2: act(B("NVO", V, 2 * V), ind(B("TE", 0, 912), DU("o%d" % t)))
        mm(B("PA", 0, V), B("LOA", 0, 128), B("OG", 0, V), True, True)
        act(B("OA", 0, V), B("PA", 0, V), bias=1.0)

    def F1c(t):
        s = str(t)
        if t < 2: dist(B("PJ", 0, 56), "LWE0", "NVO", 0, 16, 56)
        tt(B("INL", 0, V), ind(B("GF", 0, 464), DU("e" + s)), B("OA", 0, V), A.is_equal)
        dist(B("PJ", 64, 92), "LW", "INL", 0, 16, 28)

    def F1k(t):
        act(B("KV", 0, V), ind(B("KC", 0, 464), DU("kc%d" % t)))
        dist(B("PJ", 128, 156), "LWE1" if t == 0 else "LWE0", "KV", 0, 16, 28)

    def F2(t):
        s, par = str(t), t & 1
        jo, pa, kv = DF("jo" + s), DF("pa" + s), DF("kv" + s)
        ts(DF("ow" + s), DN("o" + s), 448.0, A.is_lt)
        ts(jo, B("PJ", 64, 92), 0.5, A.is_lt)
        tt(jo, jo, DF("ow" + s), A.mult)
        if t < 2:
            ts(DN("pa" + s), DN("o" + s), 1, A.bitwise_and)
            ts(pa, DN("pa" + s), float(1 - par), A.is_equal)
            tt(pa, pa, jo, A.mult)
            ts(DF("nf" + s), B("PJ", 0, 28), 255.0, A.is_lt)
            tt(pa, pa, DF("nf" + s), A.mult)
            ts(kv, B("PJ", 128, 156), 128.0, A.add)
            tt(kv, B("PJ", 28, 56), kv, A.is_gt)
            tt(pa, pa, kv, A.mult)
            ts(pa, pa, 128.0, A.mult)
            ts(jo, jo, 64.0, A.mult)
            tt(DB("fl"), jo, pa, A.add)
        else: ts(DB("fl"), jo, 64.0, A.mult)
        mm(B("PA", 0, V), B("IP", 0, 128), B("OG", 0, V), True, False)
        spread(DB("fl"), False)
        act(B("PAY", 0, V), B("PA", 0, V))

    def F3(t):
        u = DU("ps%d" % t)
        emit("v", [("WP", 0, WIN)], [("PAY", 0, V)] + u[1], lambda: g.vector.tensor_copy(T["WP"][:, 0:WIN].indirect(u[0]), T["PAY"][:, 0:V]))

    it = lambda k, n=32: B("IT", 32 * k, 32 * k + n, 1, 112)
    ii = lambda k: B("II", 32 * k, 32 * k + 32, 1, 112)

    def injuries(t):
        s = str(t)
        scan(B("SC", 0, 512, 1, 112), B("RM", 0, 512, 1, 112), B("PK", 0, 512, 1, 112), A.mult, A.max)
        top = B("SC", 15, 512, 16, 112)
        cp(ii(0), top)
        tt(it(0), top, B("TH0" if t == 0 else "THC", 0, 32, 1, 112), A.is_gt)
        ts(ii(1), ii(0), 63, A.bitwise_and)
        ts(it(2), ii(1), 28.0, A.is_ge)
        ib, ib0, ib1 = B("IB", 0, 32, 1, 112), B("IB", 0, 16, 1, 112), B("IB", 16, 32, 1, 112)
        tt(ib, it(2), it(0), A.mult)
        up, on = B("UPR", 0, 112, 1, 112), B("ONE", 0, 112, 1, 112)
        mm(P4("PN", 0, 112, 0, 16), up, ib0, True, True)
        mm(P4("PN", 0, 112, 16, 32), up, ib1, True, False)
        mm(P4("PN", 0, 112, 16, 32), on, ib0, False, True)
        tt(B("OHP", 0, 256), ind(B("II", 32, 64), B("LP", 0, 16)), B("PATP", 0, 256), A.is_equal)
        tt(it(3), ib, ii(1), A.mult)
        ts(it(4), P4("PN", 0, 112, 0, 32), float(CAP), A.is_lt)
        tt(it(5), it(4), it(3), A.mult)
        tt(B("OHC", 0, V), ind(B("IT", 160, 192), B("LC", 0, 28)), B("PATC", 0, V), A.is_equal)
        for q in range(4):
            for h in range(2):
                b = h * 8 + 2 * q
                mm(P4("PN", 32 * q, 32 * q + 32, 64, 120), B("OHP", b * 16, b * 16 + 32), B("OHC", b * 28, b * 28 + 56), h == 0, h == 1)
        joins(t)
        ts(DF("n0" + s), B("PN", 64, 92), col(20), A.mult)
        ts(DF("n1" + s), B("PN", 92, 120), col(21), A.mult)
        tt(DB("cn" + s), DF("n0" + s), DF("n1" + s), A.add)
        send(B("LN" + s, 0, 32), out32("cn" + s), "rn" + s, route(rank + 1))

    def joins(t):
        par = t & 1
        tt(it(8), ii(1), B("W32", 0, 32, 1, 112), A.mult)
        tt(it(8), it(8), B("B32", 0, 32, 1, 112), A.add)
        for j in range(2 if t < 2 else 1):
            ts(ii(2 + j), ii(0), 64 << j, A.bitwise_and)
            ts(it(6 + j), ii(2 + j), 1.0, A.is_ge)
            tt(it(6 + j), it(6 + j), it(0), A.mult)
            for h in range(2):
                tt(B("XX", 32 * h + 16 * j, 32 * h + 16 * j + 16, 1, 112), B("IT", 192 + 32 * j + 16 * h, 208 + 32 * j + 16 * h, 1, 112),
                   B("IT", 256 + 16 * h, 272 + 16 * h, 1, 112), A.mult)
        for h in range(2):
            mm(P4("PJ", 0, 32, 112 * h, 112 * h + 112), B("XX", 32 * h, 32 * h + 32, 1, 112), B("IDN", 0, 112, 1, 112), True, True)
        act(P4("XT", 0, 32, 0, M), P4("PJ", 0, 32, 0, M))
        if t < 2:
            for a in range(8):
                mm(B("PJ", 480, 508), mat("EE", 2 * a + par, 32), B("XT", a, a + 217, 8, 32), a == 0, a == 7)
        mm(B("PJ", 224, 448), B("EJ", 0, 128, 1, 32), B("XT", 0, M, 1, 32), True, True)

    def next_e(t):
        s, n = str(t), str(t + 1)
        ts(DF("cq" + s), B("PJ", 480, 508), 0.0, A.is_equal)
        tt(DF("cq" + s), DF("cq" + s), DF("eb" + n), A.mult)
        tt(DF("e" + n), B("PJ", 480, 508), DF("cq" + s), A.add)

    def ghosts(t):
        s = str(t)
        tt(DN("gd" + s), B("LG%d" % (t + 1), 0, 28), DB("cn" + s), A.add)
        ts(DN("gd" + s), DN("gd" + s), 15, A.bitwise_and)
        cp(B("DT", 28, 56), DN("gd" + s))

    def own(t):
        s, n = str(t), str(t + 1)
        tt(DN("dd" + s), DN("nd" + s), B("LN" + s, 0, 28), A.add)
        ts(DN("d" + n), DN("dd" + s), 15, A.bitwise_and)
        cp(B("DT", 0, 28), DN("d" + n))

    def lists(t):
        par = t & 1
        gf = B("GF", 1 + par, 448 + par, 2)
        tt(B("UPD", 0, M), B("PJ", 224, 448), B("OHN", 0, M), A.mult)
        tt(gf, gf, B("UPD", 0, M), A.add)
        if t < 2: ts(B("G0", par, V - 1 + par, 2), gf, 0.5, A.is_gt)
        if t == 0: cp(B("GU", 0, M), gf)

    def count1(t):
        cp(B("CB", 0, 32, 1, 112), it(0))
        mm(B("PN", 128, 160), B("ONE", 0, 128, 1, 112), B("CB", 0, 32, 1, 112), True, True)

    def count2(t):
        for j in range(2):
            lo = 128 + 16 * j
            emit("v", [("CF", 0, 2)], [("PN", 0, 512)], lambda: g.vector.tensor_reduce(T["CF"][:, j:j + 1], T["PN"][:, lo:lo + 8], AxisListType.X, A.add))
        tt(B("CI", 0, 1), B("CF", 0, 1), B("CF", 1, 2), A.add)
        ts(B("CI", 1, 2), B("CI", 0, 1), 31, A.bitwise_and)
        ts(B("CF", 2, 3), B("CI", 1, 2), 4096.0, A.mult)
        ts(B("THC", 0, 32, 1, 112), B("TH0", 0, 32, 1, 112), B("CF", 2, 3, 1, 112), A.add)

    SF = lambda k: B("SF", k * M, k * M + M)
    SI = B("SI", 0, M)

    def sp0(t):
        mm(B("PN", 256, 480), B("BD", 0, 128), B("G0", t & 1, V - 1 + (t & 1), 2), True, True)
        ts(B("OHN", 0, M), B("PN", 256, 480), col(0), A.is_equal)

    def spS(t):
        gf = B("GF", 1 + (t & 1), 448 + (t & 1), 2)
        act(SF(0), gf, bias=col(28))
        act(SF(3), gf, scale=2.0, bias=col(29))
        act(SF(4), gf, scale=-8192.0, bias=col(30), relu=True)

    def spV(t):
        par = t & 1
        tt(SI, SF(0), B("S1", par * M, par * M + M), A.mult)
        ts(SI, SI, 4, A.arith_shift_right)
        tt(SF(1), SI, SF(0), A.add)

    def slots1(t, j):
        par = t & 1
        dist(B("PS", 112 * j, 112 * j + 112), "LWD", "KW", par * CELLS + j * CH, 16, 112)
        if j: mm(B("PS", 256, 480), B("R2B", 0, 128), B("TN", 1 + par, 448 + par, 2), True, True)

    def slots2(t):
        par = t & 1
        tt(SF(2), B("PS", 0, M), B("S1", (2 + par) * M, (3 + par) * M), A.mult)
        tt(SF(3), B("PS", 256, 480), SF(3), A.mult)
        tt(SF(1), SF(1), SF(2), A.add)
        tt(SI, SF(1), SF(3), A.add)
        ts(SI, SI, 4095, A.bitwise_and)
        tt(SF(1), SI, SF(4), A.add)
        ts(B("ISL", 0, M), SF(1), float(W), A.min)

    def slots3(a, b):
        act(B("WR", 16 * a, 16 * b), ind(B("REC", 0, W + 16), B("ISL", a, b)), scale=0.5)

    def L1(t):
        u = DU("ps%d" % t)
        ts(B("ZH", 0, M), zin(t), 0.5, A.mult, -0.25, A.add)
        emit("v", [("WR", 0, WIN)], [("RP", 0, V)] + u[1], lambda: g.vector.tensor_copy(T["WR"][:, 0:WIN].indirect(u[0]), T["RP"][:, 0:V]))

    def L2(t, j):
        s = str(t)
        b, z = half(), j * CH // 16
        scan(B("KT", b, b + CH), B("RM", 0, CH), B("WR", j * CH, j * CH + CH), A.mult, A.max)
        tt(B("ZI", z, z + 112), B("KT", b + 15, b + CH, 16), B("ZH", z, z + 112), A.add)
        if j == 0: return
        cp(B("ZB" + s, 0, M), B("ZI", 0, M))
        send(B("LZ" + s, 0, M), B("ZB" + s, 0, M), "rz" + s, route(rank + 1 + t))

    def thresholds1():
        ts(B("IOQ", 3, 4), B("IOQ", 0, 1), 7, A.bitwise_and)
        ts(B("IOQ", 4, 5), B("IOQ", 2, 3), 1, A.bitwise_and)
        cp(col(21), B("IOQ", 4, 5))
        ts(col(20), col(21), -1.0, A.mult, 1.0, A.add)
        cp(col(22), B("IOQ", 0, 1))
        cp(col(23), B("IOQ", 3, 4))
        ts(B("THT", 0, M, 1, 8), B("THI", 0, M, 1, 8), 4, A.arith_shift_right)
        ts(B("THT", M, 2 * M, 1, 8), B("THI", 0, M, 1, 8), 15, A.bitwise_and)
        cp(B("THB", 0, 2 * M, 1, 8), B("THT", 0, 2 * M, 1, 8))
        ts(B("SELT", 0, 16), B("IO8", 0, 16), col(22), A.is_equal)
        ts(B("SELU", 0, 16), B("SELT", 0, 16), 16.0, A.mult)
        for h in range(2):
            o = P4("PN", 0, 112, 16 * h, 16 * h + 16)
            mm(o, B("THB", 112 * h, 112 * h + 112, 1, 8), B("SELU", 0, 16, 1, 8), True, False)
            mm(o, B("THB", M + 112 * h, M + 112 * h + 112, 1, 8), B("SELT", 0, 16, 1, 8), False, True)
        cp(B("LP", 0, 16), B("LPI", 0, 16))
        ts(DN("hg"), aD, 1.0 / 28, A.mult, 0.5 / 28 - 0.5, A.add)
        ts(DN("h3"), DN("hg"), 3, A.arith_shift_right)
        ts(DF("h8"), DN("h3"), 8.0, A.mult)
        tt(DF("h8"), DF("h8"), DN("hg"), A.add)
        cp(B("LC", 0, 28), DF("h8"))

    def thresholds2(): ts(B("TH0", 0, 32, 1, 112), P4("PN", 0, 112, 0, 32), 4096.0, A.mult, 4095.0, A.add)

    def join_mats():
        fill(B("W32", 0, 32), 1.0)
        fill(B("B32", 0, 32), 1.0)
        for h in (0, 16):
            fill(B("W32", h, h + 8), 16.0)
            fill(B("B32", h, h + 8), 0.0)
        ts(col(24), col(22), 15.5, A.is_gt)
        ts(col(25), col(22), 15.5, A.is_lt)
        ts(B("EJ", 0, 128, 1, 32), B("IOM", 0, 128, 1, 32), col(23, 32), A.is_equal, col(25, 32), A.mult)
        ts(B("EE0", 0, 128, 1, 32), B("IOM", 0, 128, 1, 32), col(23, 32), A.is_equal, col(24, 32), A.mult)
        for a in range(8): cp(B("EE", 16 * a, 16 * a + 129 * 15 + 1, 129, 32), B("EE0", 16 * a, 16 * a + 16, 1, 32))

    slots1(0, 0)
    slots1(0, 1)
    base1("LWE0")
    fill(B("GF", 0, 1), -5.0)
    fill(B("GF", V + 1, 464), -5.0)
    ts(B("GF", 1, V + 1), B("GI", 0, V), 1.0, A.add)
    ts(B("IOQ", 6, 7), B("IOQ", 0, 1), 1, A.add)
    ts(B("IOQ", 7, 8), B("IOQ", 6, 7), 15, A.bitwise_and)
    cp(col(26), B("IOQ", 7, 8))
    ts(B("ID", 0, 912), B("SF", 0, 912), col(26), A.is_equal)
    fill(B("DT", 56, 64), 0.0)
    ts(B("NBT", 0, V), B("NBI", 0, V), 4, A.arith_shift_right)
    ts(B("NBT", V, 2 * V), B("NBI", 0, V), 15, A.bitwise_and)
    base2("0")
    act(B("LWO", 0, 2048), B("LW", 0, 2048), scale=col(9))
    dist(B("PD", 0, 28), "LWD", "TN", 1, 16, 28)
    cp(B("NBD", 0, V), B("NBT", 0, V))
    cp(B("NBD", V, 2 * V), B("NBT", V, 2 * V))
    dma("y", (T["NW"][0:113:16, 0:7168], [("NW", 0, 7168)]), B("NBD", 0, V))
    dma("y", (T["NW"][1:114:16, 0:7168], [("NW", 0, 7168)]), B("NBD", V, 2 * V))
    for t in range(3):
        fill(out32("mv%d" % t), 0.0)
        fill(out32("cn%d" % t), 0.0)
    base3("0", DF("e0"))
    E1(0)
    cp(B("DT", 0, 28), B("PD", 0, 28))
    cp(DN("d0"), B("PD", 0, 28))
    cp(DB("mv0"), B("PD", 0, 28))
    iota(B("CK", 0, 512), [[0, 32], [-256, 16]], 3840, 0)
    send_moved(0)
    iota(B("PATP", 0, 256), [[0, 16], [1, 16]], 0, 0)
    iota(B("PATC", 0, V), [[0, 16], [1, 28]], 28, 0)
    iota(B("LPI", 0, 16), [[16, 2], [1, 8]], 8, 0)
    asel(B("UPR", 0, 112), B("ONE", 0, 112), [[1, 112]], A.is_gt, 0, -1)
    E2(0)
    ze(0)
    D1(0)
    E3(0)
    act(B("LW4", 0, 2048), B("LW", 0, 2048), scale=4.0)
    fill(B("REC", W, W + 16), 0.0)
    for j in range(3): fill(B("J84", 28 * j, 28 * j + 28), float(j))
    act(B("TE", 0, 912), B("WD0", 0, 912))
    ts(B("LOA", 0, 128), B("BD", 0, 128), col(9), A.mult)
    ts(B("IP", 0, 128), B("IDN", 0, 128), col(17), A.mult)
    F1(0)
    D2(0)
    R1(0, 0)
    E4(0)
    R1(0, 1)
    E5a(0)
    R1(0, 2)
    R1x(0)
    F1b(0)
    E5b(0)
    cp(B("DT", 28, 56), B("LG0", 0, 28))
    D3(0)
    sp0(0)
    F1k(0)
    F1c(0)
    base1("LWE1")
    spS(0)
    spV(0)
    slots2(0)
    act(B("DA2", 0, 2048), B("WD0", 0, 2048))
    act(B("EE", 0, 2048, 1, 32), B("WD0", 0, 2048, 1, 32))
    asel(B("DA2", 2, 2035, 16), B("ONE", 0, 128), [[-1, 16], [-16, 8]], A.is_equal, 0, 1)
    iota(B("IO8", 0, 16), [[0, 2], [1, 8]], 0, 0)
    act(B("IT", 0, 448), B("WD0", 0, 448))
    fill(B("II", 0, 128), 0.0)
    act(B("RM", 0, CH), B("RA", 0, CH), relu=True)
    base2("1")
    D4(0)
    slots3(0, 56)
    slots3(56, 112)
    R2(0)
    thresholds1()
    F2(0)
    R3(0)
    slots3(112, 168)
    slots3(168, 224)
    F3(0)
    thresholds2()
    ts(B("SELD", 0, 8), B("BD", 0, 113, 16), 4096.0, A.mult)
    ts(B("SELD", 8, 16), B("BD", 0, 113, 16), 4096.0, A.mult)
    ts(col(18), col(4), col(6), A.add)
    ts(col(19), col(5), col(6), A.add)
    ts(B("SELP", 0, 8), B("BD", 0, 113, 16), col(18), A.mult)
    ts(B("SELP", 8, 16), B("BD", 0, 113, 16), col(19), A.mult)
    open_keys()
    keys("WD0", "SELD", False)
    keys("WP", "SELP", True)
    join_mats()
    base3("1", DF("eb1"))
    for t in range(3):
        if t == 0: L1(0)
        injuries(t)
        if t == 1: base3("2", DF("eb2"))
        if t > 0: L1(t)
        if t == 2: break
        n = t + 1
        h = n & 1
        next_e(t)
        E1(n)
        if n == 1:
            lists(0)
            table(False)
            sp0(1)
            sgather(0, 56)
            sgather(56, 112)
        F1(n)
        if n == 1: spS(1)
        count1(t)
        L2(t, 0)
        L2(t, 1)
        own(t)
        D1(n)
        table(True, n == 2)
        ghosts(t)
        E2(n)
        D2(n)
        ze(n)
        E3(n)
        if n == 2:
            lists(1)
            spS(2)
        spV(n)
        sgather(224 * h, 224 * h + 56)
        R1(n, 0)
        E5a(n)
        R1(n, 1)
        R1(n, 2)
        R1x(n)
        E4(n)
        F1b(n)
        sgather(224 * h + 56, 224 * h + 112)
        sgather(224 * h + 112, 224 * h + 168)
        E5b(n)
        D3(n)
        F1c(n)
        if n == 2: F2(2)
        slots1(n, 0)
        D4(n)
        R2(n)
        sgather(224 * h + 168, 224 * h + 224)
        open_keys()
        if n == 2:
            F3(2)
            keys("WP", "SELP", False)
        slots1(n, 1)
        R3(n)
        if n == 1:
            keys("WD1", "SELD", False)
            scans(CELLS, 2 * CELLS)
            F1k(1)
        else: keys("WD2", "SELD", True)
        slots2(n)
        count2(t)
        if n == 2: sp0(2)
        if n == 1:
            vgather(168, 224)
            sgather(112, 168)
        else: ts(B("WR", 16 * 168, CELLS), ind(B("REC", 0, W + 16), B("ISL", 168, 224)), 0.5, A.mult)
        slots3(0, 56)
        if n == 1: F2(1)
        slots3(56, 112)
        if n == 1: scans(0, CELLS)
        slots3(112, 168)
        if n == 1:
            slots3(168, 224)
            F3(1)
            base1("LWE0")
            keys("WP", "SELP", True)
            base2("2")
    L2(2, 0)
    L2(2, 1)
    own(2)
    spread(B("DT", 0, 28), True)
    lists(2)
    ts(B("YL", 0, V), B("GF", 1, V + 1), -1.0, A.add)
    dma("y", (T.yl[:, :], []), B("YL", 0, V))
    act(B("YD", 0, V), B("PA", 0, V))
    dma("y", (T.yd[:, :], []), (T["SF"][2:115:16, 0:V], [("SF", 0, V)]))
    dma("y", (T.yz[:, :], []), B("LZ2", 0, M))
    finish()
